import numpy as np
import ml_dtypes

BF16 = ml_dtypes.bfloat16


def bf(x):
    return np.asarray(x, np.float32).astype(BF16)


def f32(x):
    return np.asarray(x, np.float32)


def f64(x):
    return np.asarray(x).astype(np.float64)


def striped(idx):
    return np.concatenate([l.reshape(-1, 16).T for l in idx])


def rows(idx, k):
    return np.tile(np.repeat(idx, 16, axis=0), (k // (16 * 8), 1))


def look(tab, idx):
    return np.take_along_axis(f64(tab), rows(idx, len(tab)), axis=1)


K, S, V, N, M = 256, 2048, 1024, 1024, 128


def silu(v):
    return v / (1.0 + np.exp(-v))


def setup_inputs():
    return {"tab": f32(np.random.standard_normal((K, S))), "y": f32(np.random.standard_normal((K, V))), "w": bf(np.random.standard_normal((K, M)) / np.sqrt(K)), "b": f32(0.5 * np.random.standard_normal((M, 1))), "offs": striped(np.stack([np.random.permutation(S)[:N] for _ in range(8)]))}


def reference(tab, y, w, b, offs):
    idx = np.stack([g.T.reshape(-1) for g in np.split(offs, 8)])
    t = look(tab, idx)
    x = silu(t) * f64(y)
    y = f64(w).T @ x
    return np.maximum(y + f64(b), 0.0)

@@ -1,0 +1,50 @@
+import concourse.mybir as mybir
+
+F32, BF16, U16 = mybir.dt.float32, mybir.dt.bfloat16, mybir.dt.uint16
+SILU = mybir.ActivationFunctionType.Silu
+ADD, MAX, MULT = mybir.AluOpType.add, mybir.AluOpType.max, mybir.AluOpType.mult
+
+P = 128
+ROWS, S, N, M = 256, 2048, 1024, 128
+BLOCKS = ROWS // P
+PIECE = 512
+PIECES = N // PIECE
+
+FLOPS = 2 * ROWS * N * M
+
+
+def tile_lookup_gate_silu_relu_kernel(tc, tab, y, w, b, offs, out):
+    nc = tc.nc
+    with (
+        tc.tile_pool(name="held", bufs=1) as held,
+        tc.tile_pool(name="work", bufs=2) as work,
+        tc.psum_pool(name="psum", bufs=1) as psum,
+    ):
+        offsets = held.tile([P, N // 16], U16, name="offsets")
+        nc.sync.dma_start(offsets[:], offs)
+        tables = [held.tile([P, S], F32, name=f"table{r}") for r in range(BLOCKS)]
+        streams = [held.tile([P, N], F32, name=f"stream{r}") for r in range(BLOCKS)]
+        for r in range(BLOCKS):
+            nc.sync.dma_start(tables[r][:], tab[r * P : (r + 1) * P, :])
+        for r in range(BLOCKS):
+            nc.sync.dma_start(streams[r][:], y[r * P : (r + 1) * P, :])
+        weights = held.tile([P, BLOCKS, M], BF16, name="weights")
+        nc.gpsimd.dma_start(weights[:], w.rearrange("(r p) m -> p r m", p=P))
+        bias = held.tile([P, 1], F32, name="bias")
+        nc.gpsimd.dma_start(bias[:], b)
+
+        sums = [psum.tile([P, PIECE], F32, name=f"sum{h}") for h in range(PIECES)]
+        for r in range(BLOCKS):
+            for h in range(PIECES):
+                columns = slice(h * PIECE, (h + 1) * PIECE)
+                entries = offsets[:, h * PIECE // 16 : (h + 1) * PIECE // 16]
+                gate = work.tile([P, PIECE], F32, name="gate")
+                nc.scalar.activation(gate[:], tables[r][:].indirect(entries), SILU)
+                x = work.tile([P, PIECE], BF16, name="x")
+                nc.vector.tensor_tensor(x[:], gate[:], streams[r][:, columns], MULT)
+                nc.tensor.matmul(sums[h][:], weights[:, r, :], x[:], start=r == 0, stop=r == BLOCKS - 1)
+
+        for h in range(PIECES):
+            result = work.tile([P, PIECE], F32, name="result")
+            nc.vector.tensor_scalar(result[:], sums[h][:], bias[:], 0.0, ADD, MAX)
+            nc.sync.dma_start(out[:, h * PIECE : (h + 1) * PIECE], result[:])

@@ -20,6 +20,11 @@ def tile_lookup_gate_silu_relu_kernel(tc, tab, y, w, b, offs, out):
         tc.tile_pool(name="work", bufs=2) as work,
         tc.psum_pool(name="psum", bufs=1) as psum,
     ):
+        zero = held.tile([P, 1], F32, name="zero")
+        nc.vector.memset(zero[:], 0.0)
+        warm = held.tile([P, 1], F32, name="warm")
+        nc.scalar.activation(warm[:], zero[:], SILU)
+
         offsets = held.tile([P, N // 16], U16, name="offsets")
         nc.sync.dma_start(offsets[:], offs)
         tables = [held.tile([P, S], F32, name=f"table{r}") for r in range(BLOCKS)]

@@ -2,6 +2,7 @@ import concourse.mybir as mybir
 
 F32, BF16, U16 = mybir.dt.float32, mybir.dt.bfloat16, mybir.dt.uint16
 SILU = mybir.ActivationFunctionType.Silu
+RELU = mybir.ActivationFunctionType.Relu
 ADD, MAX, MULT = mybir.AluOpType.add, mybir.AluOpType.max, mybir.AluOpType.mult
 
 P = 128
@@ -9,6 +10,8 @@ ROWS, S, N, M = 256, 2048, 1024, 128
 BLOCKS = ROWS // P
 PIECE = 512
 PIECES = N // PIECE
+CHUNK = PIECE // 2
+CHUNKS = N // CHUNK
 
 FLOPS = 2 * ROWS * N * M
 
@@ -17,7 +20,7 @@ def tile_lookup_gate_silu_relu_kernel(tc, tab, y, w, b, offs, out):
     nc = tc.nc
     with (
         tc.tile_pool(name="held", bufs=1) as held,
-        tc.tile_pool(name="work", bufs=2) as work,
+        tc.tile_pool(name="work", bufs=4) as work,
         tc.psum_pool(name="psum", bufs=1) as psum,
     ):
         zero = held.tile([P, 1], F32, name="zero")
@@ -28,28 +31,36 @@ def tile_lookup_gate_silu_relu_kernel(tc, tab, y, w, b, offs, out):
         offsets = held.tile([P, N // 16], U16, name="offsets")
         nc.sync.dma_start(offsets[:], offs)
         tables = [held.tile([P, S], F32, name=f"table{r}") for r in range(BLOCKS)]
-        streams = [held.tile([P, N], F32, name=f"stream{r}") for r in range(BLOCKS)]
         for r in range(BLOCKS):
             nc.sync.dma_start(tables[r][:], tab[r * P : (r + 1) * P, :])
-        for r in range(BLOCKS):
-            nc.sync.dma_start(streams[r][:], y[r * P : (r + 1) * P, :])
         weights = held.tile([P, BLOCKS, M], BF16, name="weights")
-        nc.gpsimd.dma_start(weights[:], w.rearrange("(r p) m -> p r m", p=P))
+        nc.sync.dma_start(weights[:], w.rearrange("(r p) m -> p r m", p=P))
         bias = held.tile([P, 1], F32, name="bias")
-        nc.gpsimd.dma_start(bias[:], b)
-
-        sums = [psum.tile([P, PIECE], F32, name=f"sum{h}") for h in range(PIECES)]
+        nc.sync.dma_start(bias[:], b)
+        streams = [held.tile([P, N], F32, name=f"stream{r}") for r in range(BLOCKS)]
         for r in range(BLOCKS):
             for h in range(PIECES):
                 columns = slice(h * PIECE, (h + 1) * PIECE)
-                entries = offsets[:, h * PIECE // 16 : (h + 1) * PIECE // 16]
-                gate = work.tile([P, PIECE], F32, name="gate")
-                nc.scalar.activation(gate[:], tables[r][:].indirect(entries), SILU)
-                x = work.tile([P, PIECE], BF16, name="x")
-                nc.vector.tensor_tensor(x[:], gate[:], streams[r][:, columns], MULT)
-                nc.tensor.matmul(sums[h][:], weights[:, r, :], x[:], start=r == 0, stop=r == BLOCKS - 1)
+                nc.sync.dma_start(streams[r][:, columns], y[r * P : (r + 1) * P, columns])
 
-        for h in range(PIECES):
-            result = work.tile([P, PIECE], F32, name="result")
-            nc.vector.tensor_scalar(result[:], sums[h][:], bias[:], 0.0, ADD, MAX)
-            nc.sync.dma_start(out[:, h * PIECE : (h + 1) * PIECE], result[:])
+        sums = [psum.tile([P, CHUNK], F32, name=f"sum{k}") for k in range(CHUNKS)]
+        for r in range(BLOCKS):
+            for h in range(PIECES):
+                gate = work.tile([P, PIECE], F32, name="gate")
+                entries = offsets[:, h * PIECE // 16 : (h + 1) * PIECE // 16]
+                nc.scalar.activation(gate[:], tables[r][:].indirect(entries), SILU)
+                for c in range(PIECE // CHUNK):
+                    k = h * (PIECE // CHUNK) + c
+                    x = work.tile([P, CHUNK], BF16, name="x")
+                    nc.vector.tensor_tensor(
+                        x[:], gate[:, c * CHUNK : (c + 1) * CHUNK], streams[r][:, k * CHUNK : (k + 1) * CHUNK], MULT
+                    )
+                    nc.tensor.matmul(sums[k][:], weights[:, r, :], x[:], start=r == 0, stop=r == BLOCKS - 1)
+
+        for k in range(CHUNKS):
+            result = work.tile([P, CHUNK], F32, name="result")
+            if k % 2 == 0:
+                nc.scalar.activation(result[:], sums[k][:], RELU, bias=bias[:])
+            else:
+                nc.vector.tensor_scalar(result[:], sums[k][:], bias[:], 0.0, ADD, MAX)
+            nc.sync.dma_start(out[:, k * CHUNK : (k + 1) * CHUNK], result[:])

import concourse.mybir as mybir

F32, BF16, U16 = mybir.dt.float32, mybir.dt.bfloat16, mybir.dt.uint16
SILU = mybir.ActivationFunctionType.Silu
RELU = mybir.ActivationFunctionType.Relu
ADD, MAX, MULT = mybir.AluOpType.add, mybir.AluOpType.max, mybir.AluOpType.mult

P = 128
ROWS, S, N, M = 256, 2048, 1024, 128
BLOCKS = ROWS // P
PIECE = 512
PIECES = N // PIECE
CHUNK = PIECE // 2
CHUNKS = N // CHUNK

FLOPS = 2 * ROWS * N * M


def tile_lookup_gate_silu_relu_kernel(tc, tab, y, w, b, offs, out):
    nc = tc.nc
    with (
        tc.tile_pool(name="held", bufs=1) as held,
        tc.tile_pool(name="work", bufs=4) as work,
        tc.psum_pool(name="psum", bufs=1) as psum,
    ):
        zero = held.tile([P, 1], F32, name="zero")
        nc.vector.memset(zero[:], 0.0)
        warm = held.tile([P, 1], F32, name="warm")
        nc.scalar.activation(warm[:], zero[:], SILU)

        offsets = held.tile([P, N // 16], U16, name="offsets")
        nc.sync.dma_start(offsets[:], offs)
        tables = [held.tile([P, S], F32, name=f"table{r}") for r in range(BLOCKS)]
        for r in range(BLOCKS):
            nc.sync.dma_start(tables[r][:], tab[r * P : (r + 1) * P, :])
        weights = held.tile([P, BLOCKS, M], BF16, name="weights")
        nc.sync.dma_start(weights[:], w.rearrange("(r p) m -> p r m", p=P))
        bias = held.tile([P, 1], F32, name="bias")
        nc.sync.dma_start(bias[:], b)
        streams = [held.tile([P, N], F32, name=f"stream{r}") for r in range(BLOCKS)]
        for r in range(BLOCKS):
            for h in range(PIECES):
                columns = slice(h * PIECE, (h + 1) * PIECE)
                nc.sync.dma_start(streams[r][:, columns], y[r * P : (r + 1) * P, columns])

        sums = [psum.tile([P, CHUNK], F32, name=f"sum{k}") for k in range(CHUNKS)]
        for r in range(BLOCKS):
            for h in range(PIECES):
                gate = work.tile([P, PIECE], F32, name="gate")
                entries = offsets[:, h * PIECE // 16 : (h + 1) * PIECE // 16]
                nc.scalar.activation(gate[:], tables[r][:].indirect(entries), SILU)
                for c in range(PIECE // CHUNK):
                    k = h * (PIECE // CHUNK) + c
                    x = work.tile([P, CHUNK], BF16, name="x")
                    nc.vector.tensor_tensor(
                        x[:], gate[:, c * CHUNK : (c + 1) * CHUNK], streams[r][:, k * CHUNK : (k + 1) * CHUNK], MULT
                    )
                    nc.tensor.matmul(sums[k][:], weights[:, r, :], x[:], start=r == 0, stop=r == BLOCKS - 1)

        for k in range(CHUNKS):
            result = work.tile([P, CHUNK], F32, name="result")
            if k % 2 == 0:
                nc.scalar.activation(result[:], sums[k][:], RELU, bias=bias[:])
            else:
                nc.vector.tensor_scalar(result[:], sums[k][:], bias[:], 0.0, ADD, MAX)
            nc.sync.dma_start(out[:, k * CHUNK : (k + 1) * CHUNK], result[:])
